import numpy as np
import ml_dtypes


def mxq(x, axis, fmt="e4m3"):
    dtype, down = {"e4m3": (ml_dtypes.float8_e4m3fn, 7), "e5m2": (ml_dtypes.float8_e5m2, 14)}[fmt]
    v = np.moveaxis(np.asarray(x, np.float32).astype(ml_dtypes.bfloat16).astype(np.float64), axis, -1)
    blocks = v.reshape(v.shape[:-1] + (-1, 32))
    amax = np.abs(blocks).max(-1, keepdims=True)
    byte = np.maximum(np.where(amax > 0, np.frexp(amax)[1] - 1 + 127, 0) - down, 1)
    scale = np.exp2(byte - 127.0)
    codes = (blocks / scale).astype(np.float32).astype(dtype).astype(np.float64)
    return np.moveaxis((codes * scale).reshape(v.shape), -1, axis)


WIDE = False


def mx_kscale(k):
    if not WIDE:
        return np.ones(k)
    levels = np.array([30, -30])
    if k % 512:
        return np.exp2(np.random.permutation(np.resize(levels, k // 32))).repeat(32)
    a = np.empty((k // 512, 16))
    for p in range(k // 512):
        a[p, :8] = np.random.permutation(np.resize(levels, 8))
        for g in range(8):
            far = levels[np.abs(levels - a[p, g]) >= 10]
            a[p, g + 8] = far[np.random.randint(len(far))]
    return np.exp2(a.ravel()).repeat(32)


def f64(x):
    return np.asarray(x).astype(np.float64)


def striped(idx):
    return np.tile(np.asarray(idx).reshape(-1, 16).T, (8, 1)).astype(np.uint16)


def unstriped(offs):
    return offs[:16].T.reshape(-1).astype(np.int64)


E2M1 = np.array([0.0, 0.5, 1.0, 1.5, 2.0, 3.0, 4.0, 6.0, -0.0, -0.5, -1.0, -1.5, -2.0, -3.0, -4.0, -6.0])


def pack_weight(w, fmt):
    k, n = w.shape
    w = f64(np.asarray(w, np.float32).astype(ml_dtypes.bfloat16)).reshape(k // 32, 32, n)
    amax = np.abs(w).max(1)
    if fmt in ("e4m3", "e5m2"):
        byte = np.frexp(amax)[1] - 1 + 127 - (7 if fmt == "e4m3" else 14)
    else:
        mant, ex = np.frexp(amax / 6.0)
        byte = np.where(mant > 0.5, ex, ex - 1) + 127
    byte = np.clip(np.where(amax > 0, byte, 1), 1, 254)
    scaled = (w * np.exp2(127.0 - byte)[:, None, :]).reshape(k, n).astype(np.float32)
    by_word = np.ascontiguousarray(scaled.reshape(k // 512, 128, 4, n).transpose(0, 1, 3, 2))
    if fmt in ("e4m3", "e5m2"):
        words = by_word.astype(ml_dtypes.float8_e4m3fn if fmt == "e4m3" else ml_dtypes.float8_e5m2).view(np.uint8)
    else:
        c = by_word.astype(ml_dtypes.float4_e2m1fn).view(np.uint8) & 0xF
        words = (c[..., 0::2] | (c[..., 1::2] << 4)).reshape(k // 512, 128, 2 * n)
    return np.ascontiguousarray(words), np.ascontiguousarray(byte.astype(np.uint8).reshape(k // 512, 16, n))


def unpack_weight(words, scales, fmt):
    g, _, n = scales.shape
    words = np.ascontiguousarray(words).reshape(g, 128, n, -1)
    if fmt in ("e4m3", "e5m2"):
        vals = words.view(ml_dtypes.float8_e4m3fn if fmt == "e4m3" else ml_dtypes.float8_e5m2).astype(np.float64)
    else:
        nib = np.empty((g, 128, n, 4), np.uint8)
        nib[..., 0::2] = words & 0xF
        nib[..., 1::2] = words >> 4
        vals = E2M1[nib]
    vals = vals * np.repeat(np.exp2(scales.astype(np.float64) - 127.0), 8, axis=1)[..., None]
    return vals.transpose(0, 1, 3, 2).reshape(g * 512, n)


def sigmoid(v):
    return 1.0 / (1.0 + np.exp(-v))


def sgn(shape):
    return np.random.uniform(0.5, 2.0, shape) * np.where(np.random.standard_normal(shape) < 0, -1.0, 1.0)


K, T, J, R, F, Z, O, N, S, E = 512, 1024, 256, 512, 512, 1024, 128, 256, 1024, 1024


def setup_inputs():
    n = np.random.standard_normal
    idx = np.random.permutation(T)[:J]
    idx2 = np.random.permutation(Z)[:J]
    idx3 = np.random.permutation(J)[:O]
    idx4 = np.random.permutation(J)[:O]
    idx5 = np.random.permutation(J)[:O]
    idx6 = np.random.permutation(S)[:N]
    idx7 = np.random.permutation(E)[:O]
    ff = mx_kscale(F)
    fk = mx_kscale(K)
    fr = mx_kscale(R)
    xop = pack_weight(n((F, Z)) / ff[:, None], "e5m2")
    wp = pack_weight(n((K, R)) * 1 / np.sqrt(K) / fk[:, None], "e5m2")
    w2p = pack_weight(n((F, R)) * 1 / np.sqrt(F) * ff[:, None], "e4m3")
    vsp = pack_weight(n((R, S)) * 1 / np.sqrt(R) / fr[:, None], "e4m3")
    return {
        "xo_words": xop[0],
        "xo_scales": xop[1],
        "cq": (np.random.randint(-7, 8, (K, T)).astype(np.float64)).astype(np.float32),
        "gs": (np.random.uniform(0.1, 0.4, (K, 1)) * fk[:, None]).astype(np.float32),
        "w_words": wp[0],
        "w_scales": wp[1],
        "w2_words": w2p[0],
        "w2_scales": w2p[1],
        "sa": (np.random.uniform(0.5, 1.6, (R, 1)) * fr[:, None]).astype(np.float32),
        "sb": (np.random.uniform(0.5, 1.6, (R, 1)) * fr[:, None]).astype(np.float32),
        "sg": (sgn((R, 1))).astype(np.float32),
        "vs_words": vsp[0],
        "vs_scales": vsp[1],
        "offs": striped(idx),
        "offs2": striped(idx2),
        "offs3": striped(idx3),
        "offs4": striped(idx4),
        "offs5": striped(idx5),
        "offs6": striped(idx6),
        "offs7": striped(idx7),
    }


def reference(xo_words, xo_scales, cq, gs, w_words, w_scales, w2_words, w2_scales, sa, sb, sg, vs_words, vs_scales, offs, offs2, offs3, offs4, offs5, offs6, offs7):
    idx = unstriped(offs)
    idx2 = unstriped(offs2)
    idx3 = unstriped(offs3)
    idx4 = unstriped(offs4)
    idx5 = unstriped(offs5)
    idx6 = unstriped(offs6)
    idx7 = unstriped(offs7)
    xou = unpack_weight(xo_words, xo_scales, "e5m2")
    wu = unpack_weight(w_words, w_scales, "e5m2")
    w2u = unpack_weight(w2_words, w2_scales, "e4m3")
    vsu = unpack_weight(vs_words, vs_scales, "e4m3")
    x1 = f64(cq)[:, idx] * f64(gs)
    x1q = mxq(x1, 0, "e4m3")
    a = wu.T @ x1q
    xoidx2g = xou[:, idx2]
    b = w2u.T @ xoidx2g
    lb = b[:, 0:1]
    hid = a[:, idx3] * f64(sa) * sigmoid(a[:, idx4] * f64(sg) + lb) - b[:, idx5] * f64(sb)
    vsidx6g = vsu[:, idx6]
    hidq = mxq(hid, 0, "e5m2")
    p = vsidx6g.T @ hidq
    y = np.zeros((N, E))
    y[:, idx7] = p
    return y

@@ -1,0 +1,219 @@
+from contextlib import ExitStack
+
+import concourse.mybir as mybir
+
+K, T, J, R, F, Z, O, N, S, E = 512, 1024, 256, 512, 512, 1024, 128, 256, 1024, 1024
+FLOPS = 2 * (K * R * J + F * R * J + R * N * O)
+
+F32 = mybir.dt.float32
+BF16 = mybir.dt.bfloat16
+I32 = mybir.dt.int32
+U32 = mybir.dt.uint32
+U16 = mybir.dt.uint16
+U8 = mybir.dt.uint8
+E4M3 = mybir.dt.float8_e4m3fn_x4
+E5M2 = mybir.dt.float8_e5m2_x4
+ACT = mybir.ActivationFunctionType
+ALU = mybir.AluOpType
+
+P = 128
+PACK = 4
+QUAD = 32
+
+
+def tile_list_offsetlead_codednote_store_scattered_kernel(
+    tc, xo_words, xo_scales, cq, gs, w_words, w_scales, w2_words, w2_scales, sa, sb, sg,
+    vs_words, vs_scales, offs, offs2, offs3, offs4, offs5, offs6, offs7, out,
+):
+    nc = tc.nc
+    with ExitStack() as ctx:
+        keep = ctx.enter_context(tc.tile_pool(name="keep", bufs=1))
+        psum = ctx.enter_context(tc.psum_pool(name="psum", bufs=1))
+
+        def sb_tile(name, shape, dtype):
+            return keep.tile(shape, dtype, name=name, align_bytes=64)
+
+        def load_list(name, src):
+            tile = sb_tile(name, list(src.shape), U16)
+            nc.sync.dma_start(tile[:], src)
+            return tile
+
+        def load_words(name, src):
+            tile = sb_tile(name, [P, src.shape[2]], U32)
+            nc.sync.dma_start(tile[:].bitcast(I32), src[0].rearrange("p c t -> p (c t)").bitcast(I32))
+            return tile
+
+        def load_rows(queue, name, src):
+            tile = sb_tile(name, [P, PACK], F32)
+            queue.dma_start(tile[:], src.rearrange("(p t) one -> p (t one)", t=PACK))
+            return tile
+
+        def load_cq(t):
+            tile = sb_tile("cq%d" % t, [P, T], F32)
+            nc.sync.dma_start(tile[:], cq.rearrange("(p t) c -> t p c", t=PACK)[t])
+            return tile
+
+        def load_scales(name, src, first):
+            words = src.shape[2] // 4
+            stage = sb_tile(name + "_stage", [P, 4, words], I32)
+            plane = sb_tile(name + "_plane", [P, src.shape[2]], U8)
+            rows = 4 if first == 0 else QUAD
+            if first == 0:
+                nc.vector.memset(plane[:].bitcast(I32), 0)
+            else:
+                nc.vector.memset(stage[first : first + QUAD], 0)
+            nc.gpsimd.dma_start(
+                stage[first : first + 4], src[0].bitcast(I32).rearrange("(q r) c -> r q c", r=4)
+            )
+            for q in range(4):
+                nc.vector.tensor_copy(
+                    out=plane[QUAD * q : QUAD * q + rows, :].bitcast(I32),
+                    in_=stage[first : first + rows, q, :],
+                )
+            return plane
+
+        cq_t = [load_cq(0)]
+        l1 = load_list("l1", offs)
+        gs_t = load_rows(nc.sync, "gs_t", gs)
+        l2 = load_list("l2", offs2)
+        cq_t.append(load_cq(1))
+        cq_t.append(load_cq(2))
+        l6 = load_list("l6", offs6)
+        cq_t.append(load_cq(3))
+        w_raw = load_words("w_raw", w_words)
+        w2_raw = load_words("w2_raw", w2_words)
+        xo_raw = load_words("xo_raw", xo_words)
+        l3 = load_list("l3", offs3)
+        sa_t = load_rows(nc.sync, "sa_t", sa)
+        l4 = load_list("l4", offs4)
+        sg_t = load_rows(nc.sync, "sg_t", sg)
+        l5 = load_list("l5", offs5)
+        sb_t = load_rows(nc.sync, "sb_t", sb)
+        vs_raw = load_words("vs_raw", vs_words)
+        l7 = load_list("l7", offs7)
+
+        w_plane = load_scales("w", w_scales, 0)
+        xo_plane = load_scales("xo", xo_scales, 64)
+        w2_plane = load_scales("w2", w2_scales, 64)
+        vs_plane = load_scales("vs", vs_scales, 0)
+
+        w_sc = sb_tile("w_sc", [P, R], U8)
+        nc.vector.tensor_copy(
+            out=w_sc[:].rearrange("p (t m) -> p t m", t=PACK), in_=w_plane[:].rearrange("p (m t) -> p t m", t=PACK)
+        )
+        w2_sc = sb_tile("w2_sc", [P, R], U8)
+        nc.vector.tensor_copy(
+            out=w2_sc[:].rearrange("p (t m) -> p t m", t=PACK), in_=w2_plane[:].rearrange("p (m t) -> p t m", t=PACK)
+        )
+        xo_sc = sb_tile("xo_sc", [P, J], U8)
+        nc.vector.tensor_copy(out=xo_sc[:], in_=xo_plane[:].indirect(l2[:]))
+        vs_sc = sb_tile("vs_sc", [P, N], U8)
+        nc.vector.tensor_copy(out=vs_sc[:], in_=vs_plane[:].indirect(l6[:]))
+
+        pages = [sb_tile("page%d" % h, [P, E], F32) for h in range(N // P)]
+        for page in pages:
+            nc.vector.memset(page[:], 0.0)
+
+        x_planes = sb_tile("x_planes", [P, PACK, J], BF16)
+        for t in range(PACK):
+            nc.scalar.activation(
+                out=x_planes[:, t, :], in_=cq_t[t][:].indirect(l1[:]), func=ACT.Copy, scale=gs_t[:, t : t + 1]
+            )
+
+        w_c = sb_tile("w_c", [P, R], U32)
+        nc.scalar.copy(
+            out=w_c[:].rearrange("p (t m) -> p m t", t=PACK), in_=w_raw[:].rearrange("p (m t) -> p m t", t=PACK)
+        )
+        w2_c = sb_tile("w2_c", [P, R], U32)
+        nc.scalar.copy(
+            out=w2_c[:].rearrange("p (t m) -> p m t", t=PACK), in_=w2_raw[:].rearrange("p (m t) -> p m t", t=PACK)
+        )
+
+        x_c = sb_tile("x_c", [P, J], U32)
+        x_sc = sb_tile("x_sc", [P, J], U8)
+        half = J // 2
+        x_woven = [sb_tile("x_woven%d" % u, [P, half, PACK], BF16) for u in range(2)]
+        for u in range(2):
+            nc.vector.tensor_copy(
+                out=x_woven[u][:], in_=x_planes[:, :, u * half : (u + 1) * half].rearrange("p t j -> p j t")
+            )
+        for u in range(2):
+            cols = slice(u * half, (u + 1) * half)
+            nc.vector.quantize_mx(
+                out=x_c[:, cols].bitcast(E4M3), scales=x_sc[:, cols], in_=x_woven[u][:].rearrange("p j t -> p (j t)")
+            )
+
+        a_t = []
+        for t in range(PACK):
+            cols = slice(t * P, (t + 1) * P)
+            acc = psum.tile([P, J], F32, name="a_acc%d" % t, tag="bank%d" % t)
+            nc.tensor.matmul_mx(
+                out=acc[:], lhsT=w_c[:, cols].bitcast(E5M2), lhsT_scale=w_sc[:, cols],
+                rhs=x_c[:].bitcast(E4M3), rhs_scale=x_sc[:], start=True, stop=True,
+            )
+            rows = sb_tile("a%d" % t, [P, J], F32)
+            nc.vector.tensor_copy(out=rows[:], in_=acc[:])
+            a_t.append(rows)
+
+        xo_c = sb_tile("xo_c", [P, J], U32)
+        nc.vector.tensor_copy(out=xo_c[:], in_=xo_raw[:].indirect(l2[:]))
+        b_t = []
+        for t in range(PACK):
+            cols = slice(t * P, (t + 1) * P)
+            acc = psum.tile([P, J], F32, name="b_acc%d" % t, tag="bank%d" % (PACK + t))
+            nc.tensor.matmul_mx(
+                out=acc[:], lhsT=w2_c[:, cols].bitcast(E4M3), lhsT_scale=w2_sc[:, cols],
+                rhs=xo_c[:].bitcast(E5M2), rhs_scale=xo_sc[:], start=True, stop=True,
+            )
+            rows = sb_tile("b%d" % t, [P, J], F32)
+            nc.vector.tensor_copy(out=rows[:], in_=acc[:])
+            b_t.append(rows)
+
+        lead = [sb_tile("lead%d" % t, [P, O], F32) for t in range(PACK)]
+        gate = [sb_tile("gate%d" % t, [P, O], F32) for t in range(PACK)]
+        note = [sb_tile("note%d" % t, [P, O], F32) for t in range(PACK)]
+        gated = [sb_tile("gated%d" % t, [P, O], F32) for t in range(PACK)]
+        for t in range(PACK):
+            nc.scalar.activation(
+                out=lead[t][:], in_=a_t[t][:].indirect(l3[:]), func=ACT.Copy, scale=sa_t[:, t : t + 1]
+            )
+        for t in range(PACK):
+            nc.scalar.activation(
+                out=gate[t][:], in_=a_t[t][:].indirect(l4[:]), func=ACT.Sigmoid,
+                bias=b_t[t][:, 0:1], scale=sg_t[:, t : t + 1],
+            )
+            nc.vector.tensor_tensor(out=gated[t][:], in0=lead[t][:], in1=gate[t][:], op=ALU.mult)
+
+        vs_c = sb_tile("vs_c", [P, N], U32)
+        nc.vector.tensor_copy(out=vs_c[:], in_=vs_raw[:].indirect(l6[:]))
+
+        h_planes = sb_tile("h_planes", [P, PACK, O], BF16)
+        for t in range(PACK):
+            nc.scalar.activation(
+                out=note[t][:], in_=b_t[t][:].indirect(l5[:]), func=ACT.Copy, scale=sb_t[:, t : t + 1]
+            )
+            nc.vector.tensor_tensor(out=h_planes[:, t, :], in0=gated[t][:], in1=note[t][:], op=ALU.subtract)
+        h_woven = sb_tile("h_woven", [P, O, PACK], BF16)
+        nc.vector.tensor_copy(out=h_woven[:], in_=h_planes[:].rearrange("p t o -> p o t"))
+        h_c = sb_tile("h_c", [P, O], U32)
+        h_sc = sb_tile("h_sc", [P, O], U8)
+        nc.vector.quantize_mx(
+            out=h_c[:].bitcast(E5M2), scales=h_sc[:], in_=h_woven[:].rearrange("p o t -> p (o t)")
+        )
+
+        for h, page in enumerate(pages):
+            cols = slice(h * P, (h + 1) * P)
+            acc = psum.tile([P, O], F32, name="p_acc%d" % h, tag="bank%d" % h)
+            nc.tensor.matmul_mx(
+                out=acc[:], lhsT=vs_c[:, cols].bitcast(E4M3), lhsT_scale=vs_sc[:, cols],
+                rhs=h_c[:].bitcast(E5M2), rhs_scale=h_sc[:], start=True, stop=True,
+            )
+            p_rows = sb_tile("p%d" % h, [P, O], F32)
+            if h == 0:
+                nc.vector.tensor_copy(out=p_rows[:], in_=acc[:])
+                nc.vector.tensor_copy(out=page[:].indirect(l7[:]), in_=p_rows[:])
+                nc.sync.dma_start(out[cols, :], page[:])
+            else:
+                nc.scalar.copy(out=p_rows[:], in_=acc[:])
+                nc.scalar.activation(out=page[:].indirect(l7[:]), in_=p_rows[:], func=ACT.Copy)
+                nc.scalar.dma_start(out[cols, :], page[:])

@@ -30,8 +30,8 @@ def tile_list_offsetlead_codednote_store_scattered_kernel(
         keep = ctx.enter_context(tc.tile_pool(name="keep", bufs=1))
         psum = ctx.enter_context(tc.psum_pool(name="psum", bufs=1))
 
-        def sb_tile(name, shape, dtype):
-            return keep.tile(shape, dtype, name=name, align_bytes=64)
+        def sb_tile(name, shape, dtype, tag=None):
+            return keep.tile(shape, dtype, name=name, tag=tag or name, align_bytes=64)
 
         def load_list(name, src):
             tile = sb_tile(name, list(src.shape), U16)
@@ -43,9 +43,9 @@ def tile_list_offsetlead_codednote_store_scattered_kernel(
             nc.sync.dma_start(tile[:].bitcast(I32), src[0].rearrange("p c t -> p (c t)").bitcast(I32))
             return tile
 
-        def load_rows(queue, name, src):
+        def load_rows(name, src):
             tile = sb_tile(name, [P, PACK], F32)
-            queue.dma_start(tile[:], src.rearrange("(p t) one -> p (t one)", t=PACK))
+            nc.sync.dma_start(tile[:], src.rearrange("(p t) one -> p (t one)", t=PACK))
             return tile
 
         def load_cq(t):
@@ -53,90 +53,104 @@ def tile_list_offsetlead_codednote_store_scattered_kernel(
             nc.sync.dma_start(tile[:], cq.rearrange("(p t) c -> t p c", t=PACK)[t])
             return tile
 
-        def load_scales(name, src, first):
-            words = src.shape[2] // 4
-            stage = sb_tile(name + "_stage", [P, 4, words], I32)
-            plane = sb_tile(name + "_plane", [P, src.shape[2]], U8)
-            rows = 4 if first == 0 else QUAD
-            if first == 0:
-                nc.vector.memset(plane[:].bitcast(I32), 0)
-            else:
-                nc.vector.memset(stage[first : first + QUAD], 0)
-            nc.gpsimd.dma_start(
-                stage[first : first + 4], src[0].bitcast(I32).rearrange("(q r) c -> r q c", r=4)
-            )
+        def load_scales(name, src):
+            stage = sb_tile(name + "_stage", [4, 4, src.shape[2] // 4], I32)
+            nc.sync.dma_start(stage[:], src[0].bitcast(I32).rearrange("(q r) c -> r q c", r=4))
+            return stage
+
+        def spread_scales(name, stage, tag=None):
+            plane = sb_tile(name + "_plane", [P, 4 * stage.shape[2]], U8, tag)
+            nc.vector.memset(plane[:].bitcast(I32), 0)
             for q in range(4):
-                nc.vector.tensor_copy(
-                    out=plane[QUAD * q : QUAD * q + rows, :].bitcast(I32),
-                    in_=stage[first : first + rows, q, :],
-                )
+                nc.vector.tensor_copy(out=plane[QUAD * q : QUAD * q + 4, :].bitcast(I32), in_=stage[:, q, :])
             return plane
 
-        cq_t = [load_cq(0)]
-        l1 = load_list("l1", offs)
-        gs_t = load_rows(nc.sync, "gs_t", gs)
+        def deal_scales(name, plane):
+            dealt = sb_tile(name, [P, R], U8)
+            nc.vector.tensor_copy(
+                out=dealt[:].rearrange("p (t m) -> p t m", t=PACK), in_=plane[:].rearrange("p (m t) -> p t m", t=PACK)
+            )
+            return dealt
+
         l2 = load_list("l2", offs2)
+        xo_stage = load_scales("xo", xo_scales)
+        xo_raw = load_words("xo_raw", xo_words)
+        w2_stage = load_scales("w2", w2_scales)
+        w2_raw = load_words("w2_raw", w2_words)
+        l1 = load_list("l1", offs)
+        gs_t = load_rows("gs_t", gs)
+        cq_t = [load_cq(0)]
+        w_stage = load_scales("w", w_scales)
         cq_t.append(load_cq(1))
-        cq_t.append(load_cq(2))
         l6 = load_list("l6", offs6)
+        vs_stage = load_scales("vs", vs_scales)
+        cq_t.append(load_cq(2))
         cq_t.append(load_cq(3))
         w_raw = load_words("w_raw", w_words)
-        w2_raw = load_words("w2_raw", w2_words)
-        xo_raw = load_words("xo_raw", xo_words)
-        l3 = load_list("l3", offs3)
-        sa_t = load_rows(nc.sync, "sa_t", sa)
-        l4 = load_list("l4", offs4)
-        sg_t = load_rows(nc.sync, "sg_t", sg)
         l5 = load_list("l5", offs5)
-        sb_t = load_rows(nc.sync, "sb_t", sb)
+        sb_t = load_rows("sb_t", sb)
         vs_raw = load_words("vs_raw", vs_words)
+        l4 = load_list("l4", offs4)
+        sg_t = load_rows("sg_t", sg)
+        l3 = load_list("l3", offs3)
+        sa_t = load_rows("sa_t", sa)
         l7 = load_list("l7", offs7)
-
-        w_plane = load_scales("w", w_scales, 0)
-        xo_plane = load_scales("xo", xo_scales, 64)
-        w2_plane = load_scales("w2", w2_scales, 64)
-        vs_plane = load_scales("vs", vs_scales, 0)
-
-        w_sc = sb_tile("w_sc", [P, R], U8)
-        nc.vector.tensor_copy(
-            out=w_sc[:].rearrange("p (t m) -> p t m", t=PACK), in_=w_plane[:].rearrange("p (m t) -> p t m", t=PACK)
-        )
-        w2_sc = sb_tile("w2_sc", [P, R], U8)
-        nc.vector.tensor_copy(
-            out=w2_sc[:].rearrange("p (t m) -> p t m", t=PACK), in_=w2_plane[:].rearrange("p (m t) -> p t m", t=PACK)
-        )
-        xo_sc = sb_tile("xo_sc", [P, J], U8)
-        nc.vector.tensor_copy(out=xo_sc[:], in_=xo_plane[:].indirect(l2[:]))
-        vs_sc = sb_tile("vs_sc", [P, N], U8)
-        nc.vector.tensor_copy(out=vs_sc[:], in_=vs_plane[:].indirect(l6[:]))
 
         pages = [sb_tile("page%d" % h, [P, E], F32) for h in range(N // P)]
         for page in pages:
-            nc.vector.memset(page[:], 0.0)
+            nc.gpsimd.memset(page[:], 0.0)
 
-        x_planes = sb_tile("x_planes", [P, PACK, J], BF16)
-        for t in range(PACK):
-            nc.scalar.activation(
-                out=x_planes[:, t, :], in_=cq_t[t][:].indirect(l1[:]), func=ACT.Copy, scale=gs_t[:, t : t + 1]
-            )
-
-        w_c = sb_tile("w_c", [P, R], U32)
-        nc.scalar.copy(
-            out=w_c[:].rearrange("p (t m) -> p m t", t=PACK), in_=w_raw[:].rearrange("p (m t) -> p m t", t=PACK)
-        )
+        xo_plane = spread_scales("xo", xo_stage)
+        xo_sc = sb_tile("xo_sc", [P, J], U8)
+        nc.vector.tensor_copy(out=xo_sc[:], in_=xo_plane[:].indirect(l2[:]))
+        xo_c = sb_tile("xo_c", [P, J], U32)
+        nc.vector.tensor_copy(out=xo_c[:], in_=xo_raw[:].indirect(l2[:]))
+        w2_sc = deal_scales("w2_sc", spread_scales("w2", w2_stage))
         w2_c = sb_tile("w2_c", [P, R], U32)
         nc.scalar.copy(
             out=w2_c[:].rearrange("p (t m) -> p m t", t=PACK), in_=w2_raw[:].rearrange("p (m t) -> p m t", t=PACK)
         )
+        b_t = []
+        for t in range(PACK):
+            cols = slice(t * P, (t + 1) * P)
+            acc = psum.tile([P, J], F32, name="b_acc%d" % t, tag="bank%d" % (PACK + t))
+            nc.tensor.matmul_mx(
+                out=acc[:], lhsT=w2_c[:, cols].bitcast(E4M3), lhsT_scale=w2_sc[:, cols],
+                rhs=xo_c[:].bitcast(E5M2), rhs_scale=xo_sc[:], start=True, stop=True,
+            )
+            rows = sb_tile("b%d" % t, [P, J], F32)
+            nc.scalar.copy(out=rows[:], in_=acc[:])
+            b_t.append(rows)
+        w_sc = deal_scales("w_sc", spread_scales("w", w_stage))
+        vs_plane = spread_scales("vs", vs_stage)
+        vs_sc = sb_tile("vs_sc", [P, N], U8)
+        nc.vector.tensor_copy(out=vs_sc[:], in_=vs_plane[:].indirect(l6[:]))
+
+        x_pairs = [sb_tile("x_pair0", [P, 2, J], BF16), sb_tile("x_pair1", [P, 2, J], BF16, "xo_c")]
+        for t in range(PACK):
+            nc.scalar.activation(
+                out=x_pairs[t // 2][:, t % 2, :], in_=cq_t[t][:].indirect(l1[:]), func=ACT.Copy, scale=gs_t[:, t : t + 1]
+            )
+        w_c = sb_tile("w_c", [P, R], U32)
+        nc.scalar.copy(
+            out=w_c[:].rearrange("p (t m) -> p m t", t=PACK), in_=w_raw[:].rearrange("p (m t) -> p m t", t=PACK)
+        )
+        note = sb_tile("note", [P, PACK, O], F32, "w_raw")
+        for t in range(PACK):
+            nc.scalar.activation(
+                out=note[:, t, :], in_=b_t[t][:].indirect(l5[:]), func=ACT.Copy, scale=sb_t[:, t : t + 1]
+            )
 
         x_c = sb_tile("x_c", [P, J], U32)
         x_sc = sb_tile("x_sc", [P, J], U8)
         half = J // 2
         x_woven = [sb_tile("x_woven%d" % u, [P, half, PACK], BF16) for u in range(2)]
-        for u in range(2):
-            nc.vector.tensor_copy(
-                out=x_woven[u][:], in_=x_planes[:, :, u * half : (u + 1) * half].rearrange("p t j -> p j t")
-            )
+        for g, x_pair in enumerate(x_pairs):
+            for u in range(2):
+                nc.vector.tensor_copy(
+                    out=x_woven[u][:, :, 2 * g : 2 * g + 2],
+                    in_=x_pair[:, :, u * half : (u + 1) * half].rearrange("p t j -> p j t"),
+                )
         for u in range(2):
             cols = slice(u * half, (u + 1) * half)
             nc.vector.quantize_mx(
@@ -155,46 +169,31 @@ def tile_list_offsetlead_codednote_store_scattered_kernel(
             nc.vector.tensor_copy(out=rows[:], in_=acc[:])
             a_t.append(rows)
 
-        xo_c = sb_tile("xo_c", [P, J], U32)
-        nc.vector.tensor_copy(out=xo_c[:], in_=xo_raw[:].indirect(l2[:]))
-        b_t = []
-        for t in range(PACK):
-            cols = slice(t * P, (t + 1) * P)
-            acc = psum.tile([P, J], F32, name="b_acc%d" % t, tag="bank%d" % (PACK + t))
-            nc.tensor.matmul_mx(
-                out=acc[:], lhsT=w2_c[:, cols].bitcast(E4M3), lhsT_scale=w2_sc[:, cols],
-                rhs=xo_c[:].bitcast(E5M2), rhs_scale=xo_sc[:], start=True, stop=True,
-            )
-            rows = sb_tile("b%d" % t, [P, J], F32)
-            nc.vector.tensor_copy(out=rows[:], in_=acc[:])
-            b_t.append(rows)
-
-        lead = [sb_tile("lead%d" % t, [P, O], F32) for t in range(PACK)]
-        gate = [sb_tile("gate%d" % t, [P, O], F32) for t in range(PACK)]
-        note = [sb_tile("note%d" % t, [P, O], F32) for t in range(PACK)]
-        gated = [sb_tile("gated%d" % t, [P, O], F32) for t in range(PACK)]
-        for t in range(PACK):
-            nc.scalar.activation(
-                out=lead[t][:], in_=a_t[t][:].indirect(l3[:]), func=ACT.Copy, scale=sa_t[:, t : t + 1]
-            )
-        for t in range(PACK):
-            nc.scalar.activation(
-                out=gate[t][:], in_=a_t[t][:].indirect(l4[:]), func=ACT.Sigmoid,
-                bias=b_t[t][:, 0:1], scale=sg_t[:, t : t + 1],
-            )
-            nc.vector.tensor_tensor(out=gated[t][:], in0=lead[t][:], in1=gate[t][:], op=ALU.mult)
-
-        vs_c = sb_tile("vs_c", [P, N], U32)
+        vs_c = sb_tile("vs_c", [P, N], U32, "x_woven1")
         nc.vector.tensor_copy(out=vs_c[:], in_=vs_raw[:].indirect(l6[:]))
 
-        h_planes = sb_tile("h_planes", [P, PACK, O], BF16)
-        for t in range(PACK):
-            nc.scalar.activation(
-                out=note[t][:], in_=b_t[t][:].indirect(l5[:]), func=ACT.Copy, scale=sb_t[:, t : t + 1]
-            )
-            nc.vector.tensor_tensor(out=h_planes[:, t, :], in0=gated[t][:], in1=note[t][:], op=ALU.subtract)
+        gated = sb_tile("gated", [P, PACK, O], F32, "vs_raw")
         h_woven = sb_tile("h_woven", [P, O, PACK], BF16)
-        nc.vector.tensor_copy(out=h_woven[:], in_=h_planes[:].rearrange("p t o -> p o t"))
+        for t in range(PACK):
+            gate = sb_tile("gate%d" % t, [P, O], F32)
+            nc.scalar.activation(
+                out=gate[:], in_=a_t[t][:].indirect(l4[:]), func=ACT.Sigmoid,
+                bias=b_t[t][:, 0:1], scale=sg_t[:, t : t + 1],
+            )
+            lead = sb_tile("lead%d" % t, [P, O], F32)
+            nc.scalar.activation(
+                out=lead[:], in_=a_t[t][:].indirect(l3[:]), func=ACT.Copy, scale=sa_t[:, t : t + 1]
+            )
+            nc.vector.tensor_tensor(out=gated[:, t, :], in0=lead[:], in1=gate[:], op=ALU.mult)
+            if t % 2 == 1:
+                pair = slice(t - 1, t + 1)
+                nc.vector.tensor_tensor(
+                    out=h_woven[:, :, pair],
+                    in0=gated[:, pair, :].rearrange("p t o -> p o t"),
+                    in1=note[:, pair, :].rearrange("p t o -> p o t"),
+                    op=ALU.subtract,
+                )
+
         h_c = sb_tile("h_c", [P, O], U32)
         h_sc = sb_tile("h_sc", [P, O], U8)
         nc.vector.quantize_mx(

@@ -100,6 +100,11 @@ def tile_list_offsetlead_codednote_store_scattered_kernel(
         for page in pages:
             nc.gpsimd.memset(page[:], 0.0)
 
+        warm = sb_tile("warm", [P, 1], F32)
+        nc.vector.memset(warm[:], 0.0)
+        warm_out = sb_tile("warm_out", [P, 1], F32)
+        nc.scalar.activation(out=warm_out[:], in_=warm[:], func=ACT.Sigmoid)
+
         xo_plane = spread_scales("xo", xo_stage)
         xo_sc = sb_tile("xo_sc", [P, J], U8)
         nc.vector.tensor_copy(out=xo_sc[:], in_=xo_plane[:].indirect(l2[:]))

@@ -2,7 +2,7 @@ from contextlib import ExitStack
 
 import concourse.mybir as mybir
 
-K, T, J, R, F, Z, O, N, S, E = 512, 1024, 256, 512, 512, 1024, 128, 256, 1024, 1024
+K, T, J, R, F, O, N, S, E = 512, 1024, 256, 512, 512, 128, 256, 1024, 1024
 FLOPS = 2 * (K * R * J + F * R * J + R * N * O)
 
 F32 = mybir.dt.float32
@@ -18,7 +18,10 @@ ALU = mybir.AluOpType
 
 P = 128
 PACK = 4
-QUAD = 32
+QUADS = 4
+QUAD = P // QUADS
+LIVE = 4
+HALF = J // 2
 
 
 def tile_list_offsetlead_codednote_store_scattered_kernel(
@@ -30,91 +33,91 @@ def tile_list_offsetlead_codednote_store_scattered_kernel(
         keep = ctx.enter_context(tc.tile_pool(name="keep", bufs=1))
         psum = ctx.enter_context(tc.psum_pool(name="psum", bufs=1))
 
-        def sb_tile(name, shape, dtype, tag=None):
-            return keep.tile(shape, dtype, name=name, tag=tag or name, align_bytes=64)
+        def new_tile(name, shape, dtype, reuse=None):
+            return keep.tile(shape, dtype, name=name, tag=reuse or name, align_bytes=64)
 
         def load_list(name, src):
-            tile = sb_tile(name, list(src.shape), U16)
+            tile = new_tile(name, list(src.shape), U16)
             nc.sync.dma_start(tile[:], src)
             return tile
 
         def load_words(name, src):
-            tile = sb_tile(name, [P, src.shape[2]], U32)
+            tile = new_tile(name, [P, src.shape[2]], U32)
             nc.sync.dma_start(tile[:].bitcast(I32), src[0].rearrange("p c t -> p (c t)").bitcast(I32))
             return tile
 
-        def load_rows(name, src):
-            tile = sb_tile(name, [P, PACK], F32)
+        def load_factors(name, src):
+            tile = new_tile(name, [P, PACK], F32)
             nc.sync.dma_start(tile[:], src.rearrange("(p t) one -> p (t one)", t=PACK))
             return tile
 
         def load_cq(t):
-            tile = sb_tile("cq%d" % t, [P, T], F32)
+            tile = new_tile("cq%d" % t, [P, T], F32)
             nc.sync.dma_start(tile[:], cq.rearrange("(p t) c -> t p c", t=PACK)[t])
             return tile
 
-        def load_scales(name, src):
-            stage = sb_tile(name + "_stage", [4, 4, src.shape[2] // 4], I32)
-            nc.sync.dma_start(stage[:], src[0].bitcast(I32).rearrange("(q r) c -> r q c", r=4))
-            return stage
+        def load_scale_rows(name, src):
+            staged = new_tile(name + "_staged", [LIVE, QUADS, src.shape[2] // 4], I32)
+            nc.sync.dma_start(staged[:], src[0].bitcast(I32).rearrange("(q r) c -> r q c", r=LIVE))
+            return staged
 
-        def spread_scales(name, stage, tag=None):
-            plane = sb_tile(name + "_plane", [P, 4 * stage.shape[2]], U8, tag)
+        def spread_scale_rows(name, staged):
+            plane = new_tile(name + "_plane", [P, 4 * staged.shape[2]], U8)
             nc.vector.memset(plane[:].bitcast(I32), 0)
-            for q in range(4):
-                nc.vector.tensor_copy(out=plane[QUAD * q : QUAD * q + 4, :].bitcast(I32), in_=stage[:, q, :])
+            for q in range(QUADS):
+                nc.vector.tensor_copy(out=plane[QUAD * q : QUAD * q + LIVE, :].bitcast(I32), in_=staged[:, q, :])
             return plane
 
-        def deal_scales(name, plane):
-            dealt = sb_tile(name, [P, R], U8)
+        def deal_plane(name, plane):
+            dealt = new_tile(name, [P, R], U8)
             nc.vector.tensor_copy(
                 out=dealt[:].rearrange("p (t m) -> p t m", t=PACK), in_=plane[:].rearrange("p (m t) -> p t m", t=PACK)
             )
             return dealt
 
-        l2 = load_list("l2", offs2)
-        xo_stage = load_scales("xo", xo_scales)
-        xo_raw = load_words("xo_raw", xo_words)
-        w2_stage = load_scales("w2", w2_scales)
-        w2_raw = load_words("w2_raw", w2_words)
-        l1 = load_list("l1", offs)
-        gs_t = load_rows("gs_t", gs)
-        cq_t = [load_cq(0)]
-        w_stage = load_scales("w", w_scales)
-        cq_t.append(load_cq(1))
-        l6 = load_list("l6", offs6)
-        vs_stage = load_scales("vs", vs_scales)
-        cq_t.append(load_cq(2))
-        cq_t.append(load_cq(3))
-        w_raw = load_words("w_raw", w_words)
-        l5 = load_list("l5", offs5)
-        sb_t = load_rows("sb_t", sb)
-        vs_raw = load_words("vs_raw", vs_words)
-        l4 = load_list("l4", offs4)
-        sg_t = load_rows("sg_t", sg)
-        l3 = load_list("l3", offs3)
-        sa_t = load_rows("sa_t", sa)
-        l7 = load_list("l7", offs7)
+        def deal_words(name, words):
+            dealt = new_tile(name, [P, R], U32)
+            nc.scalar.copy(
+                out=dealt[:].rearrange("p (t m) -> p m t", t=PACK), in_=words[:].rearrange("p (m t) -> p m t", t=PACK)
+            )
+            return dealt
 
-        pages = [sb_tile("page%d" % h, [P, E], F32) for h in range(N // P)]
+        idx2 = load_list("idx2", offs2)
+        xo_staged = load_scale_rows("xo", xo_scales)
+        xo_all = load_words("xo_all", xo_words)
+        w2_staged = load_scale_rows("w2", w2_scales)
+        w2_given = load_words("w2_given", w2_words)
+        idx = load_list("idx", offs)
+        gs_t = load_factors("gs_t", gs)
+        cq_t = [load_cq(0)]
+        w_staged = load_scale_rows("w", w_scales)
+        cq_t.extend(load_cq(t) for t in range(1, PACK))
+        w_given = load_words("w_given", w_words)
+        idx5 = load_list("idx5", offs5)
+        sb_t = load_factors("sb_t", sb)
+        vs_all = load_words("vs_all", vs_words)
+        idx4 = load_list("idx4", offs4)
+        sg_t = load_factors("sg_t", sg)
+        idx3 = load_list("idx3", offs3)
+        sa_t = load_factors("sa_t", sa)
+        idx6 = load_list("idx6", offs6)
+        vs_plane = new_tile("vs_plane", [P, S], U8)
+        nc.vector.memset(vs_plane[:].bitcast(I32), 0)
+        for r in range(LIVE):
+            nc.sync.dma_start(vs_plane[r:P:QUAD, :].bitcast(I32), vs_scales[0, r : LIVE * QUADS : LIVE, :].bitcast(I32))
+        idx7 = load_list("idx7", offs7)
+
+        pages = [new_tile("page%d" % h, [P, E], F32) for h in range(N // P)]
         for page in pages:
             nc.gpsimd.memset(page[:], 0.0)
 
-        warm = sb_tile("warm", [P, 1], F32)
-        nc.vector.memset(warm[:], 0.0)
-        warm_out = sb_tile("warm_out", [P, 1], F32)
-        nc.scalar.activation(out=warm_out[:], in_=warm[:], func=ACT.Sigmoid)
-
-        xo_plane = spread_scales("xo", xo_stage)
-        xo_sc = sb_tile("xo_sc", [P, J], U8)
-        nc.vector.tensor_copy(out=xo_sc[:], in_=xo_plane[:].indirect(l2[:]))
-        xo_c = sb_tile("xo_c", [P, J], U32)
-        nc.vector.tensor_copy(out=xo_c[:], in_=xo_raw[:].indirect(l2[:]))
-        w2_sc = deal_scales("w2_sc", spread_scales("w2", w2_stage))
-        w2_c = sb_tile("w2_c", [P, R], U32)
-        nc.scalar.copy(
-            out=w2_c[:].rearrange("p (t m) -> p m t", t=PACK), in_=w2_raw[:].rearrange("p (m t) -> p m t", t=PACK)
-        )
+        xo_plane = spread_scale_rows("xo", xo_staged)
+        xo_sc = new_tile("xo_sc", [P, J], U8)
+        nc.vector.tensor_copy(out=xo_sc[:], in_=xo_plane[:].indirect(idx2[:]))
+        xo_c = new_tile("xo_c", [P, J], U32)
+        nc.vector.tensor_copy(out=xo_c[:], in_=xo_all[:].indirect(idx2[:]))
+        w2_sc = deal_plane("w2_sc", spread_scale_rows("w2", w2_staged))
+        w2_c = deal_words("w2_c", w2_given)
         b_t = []
         for t in range(PACK):
             cols = slice(t * P, (t + 1) * P)
@@ -123,71 +126,67 @@ def tile_list_offsetlead_codednote_store_scattered_kernel(
                 out=acc[:], lhsT=w2_c[:, cols].bitcast(E4M3), lhsT_scale=w2_sc[:, cols],
                 rhs=xo_c[:].bitcast(E5M2), rhs_scale=xo_sc[:], start=True, stop=True,
             )
-            rows = sb_tile("b%d" % t, [P, J], F32)
-            nc.scalar.copy(out=rows[:], in_=acc[:])
+            rows = new_tile("b%d" % t, [P, J], F32)
+            nc.vector.tensor_copy(out=rows[:], in_=acc[:])
             b_t.append(rows)
-        w_sc = deal_scales("w_sc", spread_scales("w", w_stage))
-        vs_plane = spread_scales("vs", vs_stage)
-        vs_sc = sb_tile("vs_sc", [P, N], U8)
-        nc.vector.tensor_copy(out=vs_sc[:], in_=vs_plane[:].indirect(l6[:]))
+        w_sc = deal_plane("w_sc", spread_scale_rows("w", w_staged))
 
-        x_pairs = [sb_tile("x_pair0", [P, 2, J], BF16), sb_tile("x_pair1", [P, 2, J], BF16, "xo_c")]
+        x_slices = new_tile("x_slices", [P, PACK, J], BF16)
         for t in range(PACK):
             nc.scalar.activation(
-                out=x_pairs[t // 2][:, t % 2, :], in_=cq_t[t][:].indirect(l1[:]), func=ACT.Copy, scale=gs_t[:, t : t + 1]
+                out=x_slices[:, t, :], in_=cq_t[t][:].indirect(idx[:]), func=ACT.Copy, scale=gs_t[:, t : t + 1]
             )
-        w_c = sb_tile("w_c", [P, R], U32)
-        nc.scalar.copy(
-            out=w_c[:].rearrange("p (t m) -> p m t", t=PACK), in_=w_raw[:].rearrange("p (m t) -> p m t", t=PACK)
-        )
-        note = sb_tile("note", [P, PACK, O], F32, "w_raw")
+        w_c = deal_words("w_c", w_given)
+
+        note = new_tile("note", [P, PACK, O], F32, "w_given")
         for t in range(PACK):
             nc.scalar.activation(
-                out=note[:, t, :], in_=b_t[t][:].indirect(l5[:]), func=ACT.Copy, scale=sb_t[:, t : t + 1]
+                out=note[:, t, :], in_=b_t[t][:].indirect(idx5[:]), func=ACT.Copy, scale=sb_t[:, t : t + 1]
             )
 
-        x_c = sb_tile("x_c", [P, J], U32)
-        x_sc = sb_tile("x_sc", [P, J], U8)
-        half = J // 2
-        x_woven = [sb_tile("x_woven%d" % u, [P, half, PACK], BF16) for u in range(2)]
-        for g, x_pair in enumerate(x_pairs):
+        x_c = [new_tile("x_c%d" % u, [P, HALF], U32) for u in range(2)]
+        x_sc = [new_tile("x_sc%d" % u, [P, HALF], U8) for u in range(2)]
+        x_woven = [new_tile("x_woven%d" % u, [P, HALF, PACK], BF16) for u in range(2)]
+        for pair in (slice(0, 2), slice(2, 4)):
             for u in range(2):
                 nc.vector.tensor_copy(
-                    out=x_woven[u][:, :, 2 * g : 2 * g + 2],
-                    in_=x_pair[:, :, u * half : (u + 1) * half].rearrange("p t j -> p j t"),
+                    out=x_woven[u][:, :, pair],
+                    in_=x_slices[:, pair, u * HALF : (u + 1) * HALF].rearrange("p t j -> p j t"),
                 )
         for u in range(2):
-            cols = slice(u * half, (u + 1) * half)
             nc.vector.quantize_mx(
-                out=x_c[:, cols].bitcast(E4M3), scales=x_sc[:, cols], in_=x_woven[u][:].rearrange("p j t -> p (j t)")
+                out=x_c[u][:].bitcast(E4M3), scales=x_sc[u][:], in_=x_woven[u][:].rearrange("p j t -> p (j t)")
             )
 
         a_t = []
         for t in range(PACK):
             cols = slice(t * P, (t + 1) * P)
             acc = psum.tile([P, J], F32, name="a_acc%d" % t, tag="bank%d" % t)
-            nc.tensor.matmul_mx(
-                out=acc[:], lhsT=w_c[:, cols].bitcast(E5M2), lhsT_scale=w_sc[:, cols],
-                rhs=x_c[:].bitcast(E4M3), rhs_scale=x_sc[:], start=True, stop=True,
-            )
-            rows = sb_tile("a%d" % t, [P, J], F32)
+            for u in range(2):
+                nc.tensor.matmul_mx(
+                    out=acc[:, u * HALF : (u + 1) * HALF], lhsT=w_c[:, cols].bitcast(E5M2), lhsT_scale=w_sc[:, cols],
+                    rhs=x_c[u][:].bitcast(E4M3), rhs_scale=x_sc[u][:], start=True, stop=True,
+                )
+            rows = new_tile("a%d" % t, [P, J], F32)
             nc.vector.tensor_copy(out=rows[:], in_=acc[:])
             a_t.append(rows)
 
-        vs_c = sb_tile("vs_c", [P, N], U32, "x_woven1")
-        nc.vector.tensor_copy(out=vs_c[:], in_=vs_raw[:].indirect(l6[:]))
+        vs_c = new_tile("vs_c", [P, N], U32, "w_c")
+        nc.vector.tensor_copy(out=vs_c[:], in_=vs_all[:].indirect(idx6[:]))
+        vs_sc = new_tile("vs_sc", [P, N], U8, "w_sc")
+        nc.vector.tensor_copy(out=vs_sc[:], in_=vs_plane[:].indirect(idx6[:]))
 
-        gated = sb_tile("gated", [P, PACK, O], F32, "vs_raw")
-        h_woven = sb_tile("h_woven", [P, O, PACK], BF16)
+        gated = new_tile("gated", [P, PACK, O], F32, "vs_plane")
+        h_woven = new_tile("h_woven", [P, O, PACK], BF16, "vs_all")
         for t in range(PACK):
-            gate = sb_tile("gate%d" % t, [P, O], F32)
+            gate = new_tile("gate%d" % t, [P, O], F32)
             nc.scalar.activation(
-                out=gate[:], in_=a_t[t][:].indirect(l4[:]), func=ACT.Sigmoid,
+                out=gate[:], in_=a_t[t][:].indirect(idx4[:]), func=ACT.Sigmoid,
                 bias=b_t[t][:, 0:1], scale=sg_t[:, t : t + 1],
             )
-            lead = sb_tile("lead%d" % t, [P, O], F32)
+            lead = new_tile("lead%d" % t, [P, O], F32)
             nc.scalar.activation(
-                out=lead[:], in_=a_t[t][:].indirect(l3[:]), func=ACT.Copy, scale=sa_t[:, t : t + 1]
+                out=lead[:], in_=a_t[t][:].indirect(idx3[:]), func=ACT.Copy, scale=sa_t[:, t : t + 1]
             )
             nc.vector.tensor_tensor(out=gated[:, t, :], in0=lead[:], in1=gate[:], op=ALU.mult)
             if t % 2 == 1:
@@ -198,26 +197,25 @@ def tile_list_offsetlead_codednote_store_scattered_kernel(
                     in1=note[:, pair, :].rearrange("p t o -> p o t"),
                     op=ALU.subtract,
                 )
-
-        h_c = sb_tile("h_c", [P, O], U32)
-        h_sc = sb_tile("h_sc", [P, O], U8)
+        h_c = new_tile("h_c", [P, O], U32)
+        h_sc = new_tile("h_sc", [P, O], U8)
         nc.vector.quantize_mx(
             out=h_c[:].bitcast(E5M2), scales=h_sc[:], in_=h_woven[:].rearrange("p o t -> p (o t)")
         )
 
         for h, page in enumerate(pages):
-            cols = slice(h * P, (h + 1) * P)
+            features = slice(h * P, (h + 1) * P)
             acc = psum.tile([P, O], F32, name="p_acc%d" % h, tag="bank%d" % h)
             nc.tensor.matmul_mx(
-                out=acc[:], lhsT=vs_c[:, cols].bitcast(E4M3), lhsT_scale=vs_sc[:, cols],
+                out=acc[:], lhsT=vs_c[:, features].bitcast(E4M3), lhsT_scale=vs_sc[:, features],
                 rhs=h_c[:].bitcast(E5M2), rhs_scale=h_sc[:], start=True, stop=True,
             )
-            p_rows = sb_tile("p%d" % h, [P, O], F32)
+            p_rows = new_tile("p%d" % h, [P, O], F32)
             if h == 0:
                 nc.vector.tensor_copy(out=p_rows[:], in_=acc[:])
-                nc.vector.tensor_copy(out=page[:].indirect(l7[:]), in_=p_rows[:])
-                nc.sync.dma_start(out[cols, :], page[:])
+                nc.vector.tensor_copy(out=page[:].indirect(idx7[:]), in_=p_rows[:])
+                nc.sync.dma_start(out[features, :], page[:])
             else:
                 nc.scalar.copy(out=p_rows[:], in_=acc[:])
-                nc.scalar.activation(out=page[:].indirect(l7[:]), in_=p_rows[:], func=ACT.Copy)
-                nc.scalar.dma_start(out[cols, :], page[:])
+                nc.scalar.activation(out=page[:].indirect(idx7[:]), in_=p_rows[:], func=ACT.Copy)
+                nc.scalar.dma_start(out[features, :], page[:])

from contextlib import ExitStack

import concourse.mybir as mybir

K, T, J, R, F, O, N, S, E = 512, 1024, 256, 512, 512, 128, 256, 1024, 1024
FLOPS = 2 * (K * R * J + F * R * J + R * N * O)

F32 = mybir.dt.float32
BF16 = mybir.dt.bfloat16
I32 = mybir.dt.int32
U32 = mybir.dt.uint32
U16 = mybir.dt.uint16
U8 = mybir.dt.uint8
E4M3 = mybir.dt.float8_e4m3fn_x4
E5M2 = mybir.dt.float8_e5m2_x4
ACT = mybir.ActivationFunctionType
ALU = mybir.AluOpType

P = 128
PACK = 4
QUADS = 4
QUAD = P // QUADS
LIVE = 4
HALF = J // 2


def tile_list_offsetlead_codednote_store_scattered_kernel(
    tc, xo_words, xo_scales, cq, gs, w_words, w_scales, w2_words, w2_scales, sa, sb, sg,
    vs_words, vs_scales, offs, offs2, offs3, offs4, offs5, offs6, offs7, out,
):
    nc = tc.nc
    with ExitStack() as ctx:
        keep = ctx.enter_context(tc.tile_pool(name="keep", bufs=1))
        psum = ctx.enter_context(tc.psum_pool(name="psum", bufs=1))

        def new_tile(name, shape, dtype, reuse=None):
            return keep.tile(shape, dtype, name=name, tag=reuse or name, align_bytes=64)

        def load_list(name, src):
            tile = new_tile(name, list(src.shape), U16)
            nc.sync.dma_start(tile[:], src)
            return tile

        def load_words(name, src):
            tile = new_tile(name, [P, src.shape[2]], U32)
            nc.sync.dma_start(tile[:].bitcast(I32), src[0].rearrange("p c t -> p (c t)").bitcast(I32))
            return tile

        def load_factors(name, src):
            tile = new_tile(name, [P, PACK], F32)
            nc.sync.dma_start(tile[:], src.rearrange("(p t) one -> p (t one)", t=PACK))
            return tile

        def load_cq(t):
            tile = new_tile("cq%d" % t, [P, T], F32)
            nc.sync.dma_start(tile[:], cq.rearrange("(p t) c -> t p c", t=PACK)[t])
            return tile

        def load_scale_rows(name, src):
            staged = new_tile(name + "_staged", [LIVE, QUADS, src.shape[2] // 4], I32)
            nc.sync.dma_start(staged[:], src[0].bitcast(I32).rearrange("(q r) c -> r q c", r=LIVE))
            return staged

        def spread_scale_rows(name, staged):
            plane = new_tile(name + "_plane", [P, 4 * staged.shape[2]], U8)
            nc.vector.memset(plane[:].bitcast(I32), 0)
            for q in range(QUADS):
                nc.vector.tensor_copy(out=plane[QUAD * q : QUAD * q + LIVE, :].bitcast(I32), in_=staged[:, q, :])
            return plane

        def deal_plane(name, plane):
            dealt = new_tile(name, [P, R], U8)
            nc.vector.tensor_copy(
                out=dealt[:].rearrange("p (t m) -> p t m", t=PACK), in_=plane[:].rearrange("p (m t) -> p t m", t=PACK)
            )
            return dealt

        def deal_words(name, words):
            dealt = new_tile(name, [P, R], U32)
            nc.scalar.copy(
                out=dealt[:].rearrange("p (t m) -> p m t", t=PACK), in_=words[:].rearrange("p (m t) -> p m t", t=PACK)
            )
            return dealt

        idx2 = load_list("idx2", offs2)
        xo_staged = load_scale_rows("xo", xo_scales)
        xo_all = load_words("xo_all", xo_words)
        w2_staged = load_scale_rows("w2", w2_scales)
        w2_given = load_words("w2_given", w2_words)
        idx = load_list("idx", offs)
        gs_t = load_factors("gs_t", gs)
        cq_t = [load_cq(0)]
        w_staged = load_scale_rows("w", w_scales)
        cq_t.extend(load_cq(t) for t in range(1, PACK))
        w_given = load_words("w_given", w_words)
        idx5 = load_list("idx5", offs5)
        sb_t = load_factors("sb_t", sb)
        vs_all = load_words("vs_all", vs_words)
        idx4 = load_list("idx4", offs4)
        sg_t = load_factors("sg_t", sg)
        idx3 = load_list("idx3", offs3)
        sa_t = load_factors("sa_t", sa)
        idx6 = load_list("idx6", offs6)
        vs_plane = new_tile("vs_plane", [P, S], U8)
        nc.vector.memset(vs_plane[:].bitcast(I32), 0)
        for r in range(LIVE):
            nc.sync.dma_start(vs_plane[r:P:QUAD, :].bitcast(I32), vs_scales[0, r : LIVE * QUADS : LIVE, :].bitcast(I32))
        idx7 = load_list("idx7", offs7)

        pages = [new_tile("page%d" % h, [P, E], F32) for h in range(N // P)]
        for page in pages:
            nc.gpsimd.memset(page[:], 0.0)

        xo_plane = spread_scale_rows("xo", xo_staged)
        xo_sc = new_tile("xo_sc", [P, J], U8)
        nc.vector.tensor_copy(out=xo_sc[:], in_=xo_plane[:].indirect(idx2[:]))
        xo_c = new_tile("xo_c", [P, J], U32)
        nc.vector.tensor_copy(out=xo_c[:], in_=xo_all[:].indirect(idx2[:]))
        w2_sc = deal_plane("w2_sc", spread_scale_rows("w2", w2_staged))
        w2_c = deal_words("w2_c", w2_given)
        b_t = []
        for t in range(PACK):
            cols = slice(t * P, (t + 1) * P)
            acc = psum.tile([P, J], F32, name="b_acc%d" % t, tag="bank%d" % (PACK + t))
            nc.tensor.matmul_mx(
                out=acc[:], lhsT=w2_c[:, cols].bitcast(E4M3), lhsT_scale=w2_sc[:, cols],
                rhs=xo_c[:].bitcast(E5M2), rhs_scale=xo_sc[:], start=True, stop=True,
            )
            rows = new_tile("b%d" % t, [P, J], F32)
            nc.vector.tensor_copy(out=rows[:], in_=acc[:])
            b_t.append(rows)
        w_sc = deal_plane("w_sc", spread_scale_rows("w", w_staged))

        x_slices = new_tile("x_slices", [P, PACK, J], BF16)
        for t in range(PACK):
            nc.scalar.activation(
                out=x_slices[:, t, :], in_=cq_t[t][:].indirect(idx[:]), func=ACT.Copy, scale=gs_t[:, t : t + 1]
            )
        w_c = deal_words("w_c", w_given)

        note = new_tile("note", [P, PACK, O], F32, "w_given")
        for t in range(PACK):
            nc.scalar.activation(
                out=note[:, t, :], in_=b_t[t][:].indirect(idx5[:]), func=ACT.Copy, scale=sb_t[:, t : t + 1]
            )

        x_c = [new_tile("x_c%d" % u, [P, HALF], U32) for u in range(2)]
        x_sc = [new_tile("x_sc%d" % u, [P, HALF], U8) for u in range(2)]
        x_woven = [new_tile("x_woven%d" % u, [P, HALF, PACK], BF16) for u in range(2)]
        for pair in (slice(0, 2), slice(2, 4)):
            for u in range(2):
                nc.vector.tensor_copy(
                    out=x_woven[u][:, :, pair],
                    in_=x_slices[:, pair, u * HALF : (u + 1) * HALF].rearrange("p t j -> p j t"),
                )
        for u in range(2):
            nc.vector.quantize_mx(
                out=x_c[u][:].bitcast(E4M3), scales=x_sc[u][:], in_=x_woven[u][:].rearrange("p j t -> p (j t)")
            )

        a_t = []
        for t in range(PACK):
            cols = slice(t * P, (t + 1) * P)
            acc = psum.tile([P, J], F32, name="a_acc%d" % t, tag="bank%d" % t)
            for u in range(2):
                nc.tensor.matmul_mx(
                    out=acc[:, u * HALF : (u + 1) * HALF], lhsT=w_c[:, cols].bitcast(E5M2), lhsT_scale=w_sc[:, cols],
                    rhs=x_c[u][:].bitcast(E4M3), rhs_scale=x_sc[u][:], start=True, stop=True,
                )
            rows = new_tile("a%d" % t, [P, J], F32)
            nc.vector.tensor_copy(out=rows[:], in_=acc[:])
            a_t.append(rows)

        vs_c = new_tile("vs_c", [P, N], U32, "w_c")
        nc.vector.tensor_copy(out=vs_c[:], in_=vs_all[:].indirect(idx6[:]))
        vs_sc = new_tile("vs_sc", [P, N], U8, "w_sc")
        nc.vector.tensor_copy(out=vs_sc[:], in_=vs_plane[:].indirect(idx6[:]))

        gated = new_tile("gated", [P, PACK, O], F32, "vs_plane")
        h_woven = new_tile("h_woven", [P, O, PACK], BF16, "vs_all")
        for t in range(PACK):
            gate = new_tile("gate%d" % t, [P, O], F32)
            nc.scalar.activation(
                out=gate[:], in_=a_t[t][:].indirect(idx4[:]), func=ACT.Sigmoid,
                bias=b_t[t][:, 0:1], scale=sg_t[:, t : t + 1],
            )
            lead = new_tile("lead%d" % t, [P, O], F32)
            nc.scalar.activation(
                out=lead[:], in_=a_t[t][:].indirect(idx3[:]), func=ACT.Copy, scale=sa_t[:, t : t + 1]
            )
            nc.vector.tensor_tensor(out=gated[:, t, :], in0=lead[:], in1=gate[:], op=ALU.mult)
            if t % 2 == 1:
                pair = slice(t - 1, t + 1)
                nc.vector.tensor_tensor(
                    out=h_woven[:, :, pair],
                    in0=gated[:, pair, :].rearrange("p t o -> p o t"),
                    in1=note[:, pair, :].rearrange("p t o -> p o t"),
                    op=ALU.subtract,
                )
        h_c = new_tile("h_c", [P, O], U32)
        h_sc = new_tile("h_sc", [P, O], U8)
        nc.vector.quantize_mx(
            out=h_c[:].bitcast(E5M2), scales=h_sc[:], in_=h_woven[:].rearrange("p o t -> p (o t)")
        )

        for h, page in enumerate(pages):
            features = slice(h * P, (h + 1) * P)
            acc = psum.tile([P, O], F32, name="p_acc%d" % h, tag="bank%d" % h)
            nc.tensor.matmul_mx(
                out=acc[:], lhsT=vs_c[:, features].bitcast(E4M3), lhsT_scale=vs_sc[:, features],
                rhs=h_c[:].bitcast(E5M2), rhs_scale=h_sc[:], start=True, stop=True,
            )
            p_rows = new_tile("p%d" % h, [P, O], F32)
            if h == 0:
                nc.vector.tensor_copy(out=p_rows[:], in_=acc[:])
                nc.vector.tensor_copy(out=page[:].indirect(idx7[:]), in_=p_rows[:])
                nc.sync.dma_start(out[features, :], page[:])
            else:
                nc.scalar.copy(out=p_rows[:], in_=acc[:])
                nc.scalar.activation(out=page[:].indirect(idx7[:]), in_=p_rows[:], func=ACT.Copy)
                nc.scalar.dma_start(out[features, :], page[:])
